import numpy as np
import ml_dtypes


def mxq(x, axis, fmt="e4m3"):
    dtype, down = {"e4m3": (ml_dtypes.float8_e4m3fn, 7), "e5m2": (ml_dtypes.float8_e5m2, 14)}[fmt]
    v = np.moveaxis(np.asarray(x, np.float32).astype(ml_dtypes.bfloat16).astype(np.float64), axis, -1)
    blocks = v.reshape(v.shape[:-1] + (-1, 32))
    amax = np.abs(blocks).max(-1, keepdims=True)
    byte = np.maximum(np.where(amax > 0, np.frexp(amax)[1] - 1 + 127, 0) - down, 1)
    scale = np.exp2(byte - 127.0)
    codes = (blocks / scale).astype(np.float32).astype(dtype).astype(np.float64)
    return np.moveaxis((codes * scale).reshape(v.shape), -1, axis)


WIDE = False


def mx_kscale(k):
    if not WIDE:
        return np.ones(k)
    levels = np.array([10, -10, 5, -5, 0])
    if k % 512:
        return np.exp2(np.random.permutation(np.resize(levels, k // 32))).repeat(32)
    a = np.empty((k // 512, 16))
    for p in range(k // 512):
        a[p, :8] = np.random.permutation(np.resize(levels, 8))
        for g in range(8):
            far = levels[np.abs(levels - a[p, g]) >= 10]
            a[p, g + 8] = far[np.random.randint(len(far))]
    return np.exp2(a.ravel()).repeat(32)


def f64(x):
    return np.asarray(x).astype(np.float64)


def striped(idx):
    return np.tile(idx.reshape(-1, 16).T, (8, 1)).astype(np.uint16)


def unstriped(offs):
    return offs[:16].T.reshape(-1).astype(np.int64)


def pack_weight(w):
    k, n = w.shape
    w = f64(np.asarray(w, np.float32).astype(ml_dtypes.bfloat16)).reshape(k // 32, 32, n)
    amax = np.abs(w).max(1)
    byte = np.clip(np.where(amax > 0, np.frexp(amax)[1] - 1 + 127 - 7, 1), 1, 254)
    scaled = (w * np.exp2(127.0 - byte)[:, None, :]).reshape(k, n).astype(np.float32)
    words = np.ascontiguousarray(scaled.reshape(k // 512, 128, 4, n).transpose(0, 1, 3, 2)).astype(ml_dtypes.float8_e4m3fn).view(np.uint8)
    return words, np.ascontiguousarray(byte.astype(np.uint8).reshape(k // 512, 16, n))


def unpack_weight(words, scales):
    g, p, n, _ = words.shape
    vals = np.ascontiguousarray(words).view(ml_dtypes.float8_e4m3fn).astype(np.float64) * np.repeat(np.exp2(scales.astype(np.float64) - 127.0), 8, axis=1)[..., None]
    return vals.transpose(0, 1, 3, 2).reshape(g * 512, n)


def planes(y):
    n, m = y.shape
    v = y.astype(np.float32).astype(ml_dtypes.bfloat16).astype(np.float64).reshape(n // 32, 32, m)
    top = np.abs(v).max(1)
    byte = np.clip(np.where(top > 0, np.frexp(top)[1] - 1 + 127 - 7, 1), 1, 254)
    codes = (v * np.exp2(127.0 - byte)[:, None, :]).reshape(n, m).astype(np.float32).astype(ml_dtypes.float8_e4m3fn).view(np.uint8)
    words = codes.reshape(n // 512, 128, 4, m).transpose(0, 1, 3, 2)
    return np.ascontiguousarray(words), np.ascontiguousarray(byte.astype(np.uint8).reshape(n // 512, 16, m))


K, T, S, N, W, G = 512, 2048, 512, 512, 2048, 1024


def setup_inputs():
    n = np.random.standard_normal
    s = mx_kscale(K)[:, None]
    packed_xT = pack_weight(n((K, T)) * s)
    packed_eT = pack_weight(n((K, W)) * s)
    packed_dT = pack_weight(n((K, G)) * s)
    return {
        "x_words": packed_xT[0],
        "x_scales": packed_xT[1],
        "e_words": packed_eT[0],
        "e_scales": packed_eT[1],
        "d_words": packed_dT[0],
        "d_scales": packed_dT[1],
        "wui": (n((K, N)) / np.sqrt(K) / s).astype(np.float32),
        "wuc": (n((K, N)) / np.sqrt(K) / s).astype(np.float32),
        "wiu": (n((K, N)) / np.sqrt(K) / s).astype(np.float32),
        "wic": (n((K, N)) / np.sqrt(K) / s).astype(np.float32),
        "wcu": (n((K, N)) / np.sqrt(K) / s).astype(np.float32),
        "wci": (n((K, N)) / np.sqrt(K) / s).astype(np.float32),
        "offs": striped(np.random.permutation(T)[:S]),
        "item": striped(np.random.permutation(W)[:S]),
        "cxt": striped(np.random.permutation(G)[:S]),
    }


def reference(x_words, x_scales, e_words, e_scales, d_words, d_scales, wui, wuc, wiu, wic, wcu, wci, offs, item, cxt):
    xq = unpack_weight(x_words, x_scales)[:, unstriped(offs)]
    yui = mxq(f64(wui), 0, "e4m3").T @ xq
    e_item = unpack_weight(e_words, e_scales)[:, unstriped(item)]
    yiu = mxq(f64(wiu), 0, "e4m3").T @ e_item
    yuc = mxq(f64(wuc), 0, "e4m3").T @ xq
    d_cxt = unpack_weight(d_words, d_scales)[:, unstriped(cxt)]
    ycu = mxq(f64(wcu), 0, "e4m3").T @ d_cxt
    yic = mxq(f64(wic), 0, "e4m3").T @ e_item
    yci = mxq(f64(wci), 0, "e4m3").T @ d_cxt
    out_0 = yui * yiu + yuc * ycu + yic * yci
    return (out_0,) + planes(out_0)

@@ -1,0 +1,215 @@
+from contextlib import ExitStack
+
+import concourse.mybir as mybir
+from concourse.masks import make_identity
+
+F32 = mybir.dt.float32
+BF16 = mybir.dt.bfloat16
+I32 = mybir.dt.int32
+U32 = mybir.dt.uint32
+U16 = mybir.dt.uint16
+U8 = mybir.dt.uint8
+FP8X4 = mybir.dt.float8_e4m3fn_x4
+MULT = mybir.AluOpType.mult
+
+P = 128
+PACK = 4
+K = 512
+N = 512
+S = 512
+HALF = N // 2
+WORDS = HALF // PACK
+FLOPS = 6 * 2 * K * N * S + 5 * N * S
+
+
+def tile_picked_yffm_sum_po_kernel(
+    tc, x_words, x_scales, e_words, e_scales, d_words, d_scales,
+    wui, wuc, wiu, wic, wcu, wci, offs, item, cxt, out_0, out_1, out_2,
+):
+    nc = tc.nc
+    with ExitStack() as ctx:
+        keep = ctx.enter_context(tc.tile_pool(name="keep", bufs=1))
+        psum = ctx.enter_context(tc.psum_pool(name="psum", bufs=1))
+
+        tables = {
+            "d": (d_words, d_scales, cxt, 0, nc.sync),
+            "x": (x_words, x_scales, offs, 4, nc.sync),
+            "e": (e_words, e_scales, item, 8, nc.sync),
+        }
+        pairs = [
+            ((wcu, "d"), (wuc, "x")),
+            ((wui, "x"), (wiu, "e")),
+            ((wci, "d"), (wic, "e")),
+        ]
+        steps = [(pair, factor, h) for pair in range(3) for factor in range(2) for h in range(2)]
+        last = len(steps) - 1
+        cast_on_vector = (2, 6, 11)
+        cast_on_gpsimd = ()
+
+        lists, scale_win, word_win, tok_codes, tok_scales = {}, {}, {}, {}, {}
+        for name, (words, scales, idx, row0, queue) in tables.items():
+            scale_win[name] = keep.tile([P, scales.shape[2]], U8, name=f"scale_win_{name}")
+            nc.vector.memset(scale_win[name][:].bitcast(I32), 0)
+
+        def load_list_and_scales(name):
+            words, scales, idx, row0, queue = tables[name]
+            lists[name] = keep.tile([P, S // 16], U16, name=f"list_{name}")
+            nc.sync.dma_start(lists[name][:], idx)
+            for q in range(4):
+                queue.dma_start(
+                    scale_win[name][32 * q + row0 : 32 * q + row0 + 4, :].bitcast(I32),
+                    scales[0, 4 * q : 4 * q + 4, :].bitcast(I32),
+                )
+
+        ident = keep.tile([P, P], F32, name="ident")
+        make_identity(nc, ident[:])
+
+        raw, grouped, w_codes, w_scales, held, prod = {}, {}, {}, {}, {}, {}
+
+        def load_words(name):
+            words = tables[name][0]
+            word_win[name] = keep.tile([P, words.shape[2]], U32, name=f"word_win_{name}")
+            nc.sync.dma_start(word_win[name][:].bitcast(I32), words[0].rearrange("p n t -> p (n t)").bitcast(I32))
+
+        def load_weight(k):
+            pair, factor, h = steps[k]
+            w = pairs[pair][factor][0]
+            raw[k] = keep.tile([P, PACK * HALF], F32, name=f"raw{k}", tag=f"stage{k}")
+            nc.sync.dma_start(
+                raw[k][:].rearrange("p (t m) -> p t m", t=PACK),
+                w.rearrange("(p t) m -> p t m", t=PACK)[:, :, h * HALF : (h + 1) * HALF],
+            )
+
+        words_after = {0: "d", 1: "x", 5: "e"}
+        small_after = {-1: "d", 1: "x", 3: "e"}
+        for k in range(-1, len(steps)):
+            if k >= 0:
+                load_weight(k)
+            if k in small_after:
+                load_list_and_scales(small_after[k])
+            if k in words_after:
+                load_words(words_after[k])
+
+        def gather_scales(name):
+            tok_scales[name] = keep.tile([P, S], U8, name=f"tok_scales_{name}", align_bytes=64)
+            nc.vector.tensor_copy(tok_scales[name][:], scale_win[name][:].indirect(lists[name][:]))
+
+        def gather_words(name):
+            tok_codes[name] = keep.tile([P, S], U32, name=f"tok_codes_{name}", align_bytes=64)
+            nc.vector.tensor_copy(tok_codes[name][:], word_win[name][:].indirect(lists[name][:]))
+
+        def interleave(copy, dst, src):
+            copy(dst.rearrange("p (c i t) -> p c t i", i=4, t=PACK), src.rearrange("p (t c i) -> p c t i", i=4, t=PACK))
+
+        def cast(k):
+            grouped[k] = keep.tile([P, HALF * PACK], BF16, name=f"grouped{k}", tag=f"round{k}", align_bytes=64)
+            if k in cast_on_gpsimd:
+                for c in range(2):
+                    n = HALF // 2
+                    nc.gpsimd.tensor_copy(
+                        grouped[k][:, c * n * PACK : (c + 1) * n * PACK].rearrange("p (c i t) -> p c t i", i=4, t=PACK),
+                        raw[k][:].rearrange("p (t m) -> p t m", t=PACK)[:, :, c * n : (c + 1) * n].rearrange("p t (c i) -> p c t i", i=4),
+                    )
+            else:
+                interleave(nc.vector.tensor_copy if k in cast_on_vector else nc.scalar.copy, grouped[k][:], raw[k][:])
+
+        def quantize(k):
+            w_codes[k] = keep.tile([P, HALF], U32, name=f"w_codes{k}", align_bytes=64)
+            w_scales[k] = keep.tile([P, HALF], U8, name=f"w_scales{k}", align_bytes=64)
+            nc.vector.quantize_mx(out=w_codes[k][:].bitcast(FP8X4), scales=w_scales[k][:], in_=grouped[k][:])
+
+        def project(k, jp):
+            pair, factor, h = steps[k]
+            table = pairs[pair][factor][1]
+            bank = psum.tile([P, 2, HALF], F32, name="bank", tag="bank", bufs=4)
+            for s in range(2):
+                cols = slice((2 * s + jp) * P, (2 * s + jp + 1) * P)
+                nc.tensor.matmul_mx(
+                    out=bank[:, s, :],
+                    lhsT=tok_codes[table][:, cols].bitcast(FP8X4),
+                    lhsT_scale=tok_scales[table][tables[table][3] : P, cols],
+                    rhs=w_codes[k][:].bitcast(FP8X4),
+                    rhs_scale=w_scales[k][:],
+                    start=True,
+                    stop=True,
+                )
+            return bank[:].rearrange("j s (p t) -> j t s p", t=PACK)
+
+        def dealt(tile, jp):
+            return tile[:, jp * N : (jp + 1) * N].rearrange("j (t s p) -> j t s p", t=PACK, s=2)
+
+        def use(k):
+            pair, factor, h = steps[k]
+            if factor == 0:
+                held[k] = keep.tile([P, 2 * N], F32, name=f"held{k}", tag=f"stage{k + 1 + h}")
+                for jp in range(2):
+                    nc.scalar.copy(dealt(held[k], jp), project(k, jp))
+            else:
+                tag = f"round{k + 1}" if k < last else "prod_last"
+                prod[k] = keep.tile([P, 2 * N], F32, name=f"prod{k}", tag=tag, align_bytes=64)
+                for jp in range(2):
+                    nc.vector.tensor_tensor(dealt(prod[k], jp), project(k, jp), dealt(held[k - 2], jp), MULT)
+
+        acc = {(h, jp): psum.tile([P, PACK, P], F32, name=f"acc{h}{jp}") for h in range(2) for jp in range(2)}
+        y = [keep.tile([P, PACK, 2 * P], F32, name=f"y{h}") for h in range(2)]
+        y_codes = keep.tile([P, 2 * HALF], U32, name="y_codes", align_bytes=64)
+        y_scales = keep.tile([P, 2 * HALF], U8, name="y_scales", align_bytes=64)
+        store_queue = (nc.sync, nc.scalar)
+
+        def add_up(k):
+            pair, factor, h = steps[k]
+            for jp in range(2):
+                for t in range(PACK):
+                    nc.tensor.matmul(
+                        acc[h, jp][:, t, :],
+                        lhsT=prod[k][:, jp * N + t * P : jp * N + (t + 1) * P],
+                        rhs=ident[:],
+                        is_transpose=True,
+                        start=(pair == 0 and t == 0),
+                        stop=(pair == 2 and t == PACK - 1),
+                    )
+                if pair == 2:
+                    hand_out(h, jp)
+
+        def hand_out(h, jp):
+            mine = y[h][:, :, jp * P : (jp + 1) * P]
+            nc.scalar.copy(mine, acc[h, jp][:])
+            y_grouped = keep.tile([P, P * PACK], BF16, name=f"y_grouped{h}{jp}", align_bytes=64)
+            nc.vector.tensor_copy(
+                y_grouped[:].rearrange("p (c i t) -> p c t i", i=4, t=PACK), mine.rearrange("p t (c i) -> p c t i", i=4)
+            )
+            cols = slice((2 * h + jp) * P, (2 * h + jp + 1) * P)
+            nc.vector.quantize_mx(out=y_codes[:, cols].bitcast(FP8X4), scales=y_scales[:, cols], in_=y_grouped[:])
+            if jp == 1:
+                rows = out_0[h * HALF : (h + 1) * HALF, :].rearrange("(p t) j -> p t j", t=PACK)
+                for s in range(2):
+                    store_queue[s].dma_start(rows[:, :, s * 2 * P : (s + 1) * 2 * P], y[h][s * WORDS : (s + 1) * WORDS])
+
+        gather_scales(small_after[-1])
+        for k in range(-2, len(steps) + 1):
+            if k + 2 <= last:
+                cast(k + 2)
+                if k + 2 in small_after:
+                    gather_scales(small_after[k + 2])
+                if k + 2 in words_after:
+                    gather_words(words_after[k + 2])
+            if 0 <= k + 1 <= last:
+                quantize(k + 1)
+            if 0 <= k <= last:
+                use(k)
+            if k >= 1 and steps[k - 1][1] == 1:
+                add_up(k - 1)
+
+        words_out = out_1[0].rearrange("(h p) j t -> p h (j t)", h=2).bitcast(I32)
+        for s in range(2):
+            store_queue[s].dma_start(
+                words_out[:, :, s * 2 * P : (s + 1) * 2 * P],
+                y_codes[s * WORDS : (s + 1) * WORDS, :].bitcast(I32).rearrange("p (h j) -> p h j", h=2),
+            )
+        scales_out = out_2[0].bitcast(I32).rearrange("(h r) j -> r h j", h=2)
+        for q in range(4):
+            s, b = divmod(q, 2)
+            store_queue[q % 2].dma_start(
+                scales_out[4 * b : 4 * b + 4, :, s * WORDS : (s + 1) * WORDS],
+                y_scales[32 * q : 32 * q + 4, :].bitcast(I32).rearrange("r (h j) -> r h j", h=2),
+            )

@@ -19,6 +19,7 @@ N = 512
 S = 512
 HALF = N // 2
 WORDS = HALF // PACK
+J_TILES = S // P
 FLOPS = 6 * 2 * K * N * S + 5 * N * S
 
 
@@ -32,63 +33,67 @@ def tile_picked_yffm_sum_po_kernel(
         psum = ctx.enter_context(tc.psum_pool(name="psum", bufs=1))
 
         tables = {
-            "d": (d_words, d_scales, cxt, 0, nc.sync),
-            "x": (x_words, x_scales, offs, 4, nc.sync),
-            "e": (e_words, e_scales, item, 8, nc.sync),
+            "d": (d_words, d_scales, cxt, 0),
+            "x": (x_words, x_scales, offs, 4),
+            "e": (e_words, e_scales, item, 8),
         }
-        pairs = [
-            ((wcu, "d"), (wuc, "x")),
-            ((wui, "x"), (wiu, "e")),
-            ((wci, "d"), (wic, "e")),
-        ]
-        steps = [(pair, factor, h) for pair in range(3) for factor in range(2) for h in range(2)]
-        last = len(steps) - 1
+        weights = [(wcu, "d"), (wuc, "x"), (wui, "x"), (wiu, "e"), (wci, "d"), (wic, "e")]
+        last_weight = len(weights) - 1
+        n_steps = 2 * len(weights)
         cast_on_vector = (2, 6, 11)
         cast_on_gpsimd = ()
+        split = ()
 
         lists, scale_win, word_win, tok_codes, tok_scales = {}, {}, {}, {}, {}
-        for name, (words, scales, idx, row0, queue) in tables.items():
+        for name, (words, scales, idx, row0) in tables.items():
             scale_win[name] = keep.tile([P, scales.shape[2]], U8, name=f"scale_win_{name}")
             nc.vector.memset(scale_win[name][:].bitcast(I32), 0)
-
-        def load_list_and_scales(name):
-            words, scales, idx, row0, queue = tables[name]
-            lists[name] = keep.tile([P, S // 16], U16, name=f"list_{name}")
-            nc.sync.dma_start(lists[name][:], idx)
-            for q in range(4):
-                queue.dma_start(
-                    scale_win[name][32 * q + row0 : 32 * q + row0 + 4, :].bitcast(I32),
-                    scales[0, 4 * q : 4 * q + 4, :].bitcast(I32),
-                )
 
         ident = keep.tile([P, P], F32, name="ident")
         make_identity(nc, ident[:])
 
         raw, grouped, w_codes, w_scales, held, prod = {}, {}, {}, {}, {}, {}
 
+        def load_list_and_scales(name):
+            words, scales, idx, row0 = tables[name]
+            lists[name] = keep.tile([P, S // 16], U16, name=f"list_{name}")
+            nc.sync.dma_start(lists[name][:], idx)
+            for q in range(4):
+                nc.sync.dma_start(
+                    scale_win[name][32 * q + row0 : 32 * q + row0 + 4, :].bitcast(I32),
+                    scales[0, 4 * q : 4 * q + 4, :].bitcast(I32),
+                )
+
         def load_words(name):
             words = tables[name][0]
             word_win[name] = keep.tile([P, words.shape[2]], U32, name=f"word_win_{name}")
             nc.sync.dma_start(word_win[name][:].bitcast(I32), words[0].rearrange("p n t -> p (n t)").bitcast(I32))
 
-        def load_weight(k):
-            pair, factor, h = steps[k]
-            w = pairs[pair][factor][0]
-            raw[k] = keep.tile([P, PACK * HALF], F32, name=f"raw{k}", tag=f"stage{k}")
-            nc.sync.dma_start(
-                raw[k][:].rearrange("p (t m) -> p t m", t=PACK),
-                w.rearrange("(p t) m -> p t m", t=PACK)[:, :, h * HALF : (h + 1) * HALF],
-            )
+        def load_weight(i):
+            rows = weights[i][0].rearrange("(p t) m -> p t m", t=PACK)
+            if i in split:
+                for h in range(2):
+                    part = keep.tile([P, PACK, HALF], F32, name=f"raw{i}_{h}", tag=f"stage{i}" if h == 0 else f"stage{i}b")
+                    nc.sync.dma_start(part[:], rows[:, :, h * HALF : (h + 1) * HALF])
+                    raw[2 * i + h] = part[:]
+            else:
+                whole = keep.tile([P, PACK, N], F32, name=f"raw{i}", tag=f"stage{i}")
+                nc.sync.dma_start(whole[:], rows)
+                for h in range(2):
+                    raw[2 * i + h] = whole[:].rearrange("p t (c i) -> p c t i", i=PACK)[:, :, :, 2 * h : 2 * h + 2]
 
-        words_after = {0: "d", 1: "x", 5: "e"}
-        small_after = {-1: "d", 1: "x", 3: "e"}
-        for k in range(-1, len(steps)):
-            if k >= 0:
-                load_weight(k)
-            if k in small_after:
-                load_list_and_scales(small_after[k])
-            if k in words_after:
-                load_words(words_after[k])
+        small_after = {-1: "d", 0: "x", 1: "e"}
+        words_after = {0: "d", 2: "e"}
+        words_after_small = {0: "x"}
+        for i in range(-1, len(weights)):
+            if i >= 0:
+                load_weight(i)
+            if i in words_after:
+                load_words(words_after[i])
+            if i in small_after:
+                load_list_and_scales(small_after[i])
+            if i in words_after_small:
+                load_words(words_after_small[i])
 
         def gather_scales(name):
             tok_scales[name] = keep.tile([P, S], U8, name=f"tok_scales_{name}", align_bytes=64)
@@ -98,20 +103,18 @@ def tile_picked_yffm_sum_po_kernel(
             tok_codes[name] = keep.tile([P, S], U32, name=f"tok_codes_{name}", align_bytes=64)
             nc.vector.tensor_copy(tok_codes[name][:], word_win[name][:].indirect(lists[name][:]))
 
-        def interleave(copy, dst, src):
-            copy(dst.rearrange("p (c i t) -> p c t i", i=4, t=PACK), src.rearrange("p (t c i) -> p c t i", i=4, t=PACK))
-
         def cast(k):
             grouped[k] = keep.tile([P, HALF * PACK], BF16, name=f"grouped{k}", tag=f"round{k}", align_bytes=64)
+            dst = grouped[k][:].rearrange("p (i c t) -> p c t i", i=2, t=PACK)
+            src = raw[k]
             if k in cast_on_gpsimd:
+                n = P // 2
                 for c in range(2):
-                    n = HALF // 2
-                    nc.gpsimd.tensor_copy(
-                        grouped[k][:, c * n * PACK : (c + 1) * n * PACK].rearrange("p (c i t) -> p c t i", i=4, t=PACK),
-                        raw[k][:].rearrange("p (t m) -> p t m", t=PACK)[:, :, c * n : (c + 1) * n].rearrange("p t (c i) -> p c t i", i=4),
-                    )
+                    nc.gpsimd.tensor_copy(dst[:, c * n : (c + 1) * n], src[:, c * n : (c + 1) * n])
+            elif k in cast_on_vector:
+                nc.vector.tensor_copy(dst, src)
             else:
-                interleave(nc.vector.tensor_copy if k in cast_on_vector else nc.scalar.copy, grouped[k][:], raw[k][:])
+                nc.scalar.copy(dst, src)
 
         def quantize(k):
             w_codes[k] = keep.tile([P, HALF], U32, name=f"w_codes{k}", align_bytes=64)
@@ -119,11 +122,10 @@ def tile_picked_yffm_sum_po_kernel(
             nc.vector.quantize_mx(out=w_codes[k][:].bitcast(FP8X4), scales=w_scales[k][:], in_=grouped[k][:])
 
         def project(k, jp):
-            pair, factor, h = steps[k]
-            table = pairs[pair][factor][1]
+            table = weights[k // 2][1]
             bank = psum.tile([P, 2, HALF], F32, name="bank", tag="bank", bufs=4)
             for s in range(2):
-                cols = slice((2 * s + jp) * P, (2 * s + jp + 1) * P)
+                cols = slice((2 * jp + s) * P, (2 * jp + s + 1) * P)
                 nc.tensor.matmul_mx(
                     out=bank[:, s, :],
                     lhsT=tok_codes[table][:, cols].bitcast(FP8X4),
@@ -133,83 +135,91 @@ def tile_picked_yffm_sum_po_kernel(
                     start=True,
                     stop=True,
                 )
-            return bank[:].rearrange("j s (p t) -> j t s p", t=PACK)
+            return bank[:].rearrange("j s m -> j (s m)")
 
-        def dealt(tile, jp):
-            return tile[:, jp * N : (jp + 1) * N].rearrange("j (t s p) -> j t s p", t=PACK, s=2)
+        def use(k, jps):
+            i, h = divmod(k, 2)
+            for jp in jps:
+                cols = slice(jp * N, (jp + 1) * N)
+                if i % 2 == 0:
+                    if jp == 0:
+                        tag = f"stage{i + 1}" if h == 1 else f"held{k}"
+                        held[k] = keep.tile([P, 2 * N], F32, name=f"held{k}", tag=tag)
+                    nc.scalar.copy(held[k][:, cols], project(k, jp))
+                else:
+                    if jp == 0:
+                        tag = f"round{k + 1}" if k + 1 < n_steps else "prod_last"
+                        prod[k] = keep.tile([P, 2 * N], F32, name=f"prod{k}", tag=tag, align_bytes=64)
+                    nc.vector.tensor_tensor(prod[k][:, cols], project(k, jp), held[k - 2][:, cols], MULT)
 
-        def use(k):
-            pair, factor, h = steps[k]
-            if factor == 0:
-                held[k] = keep.tile([P, 2 * N], F32, name=f"held{k}", tag=f"stage{k + 1 + h}")
-                for jp in range(2):
-                    nc.scalar.copy(dealt(held[k], jp), project(k, jp))
-            else:
-                tag = f"round{k + 1}" if k < last else "prod_last"
-                prod[k] = keep.tile([P, 2 * N], F32, name=f"prod{k}", tag=tag, align_bytes=64)
-                for jp in range(2):
-                    nc.vector.tensor_tensor(dealt(prod[k], jp), project(k, jp), dealt(held[k - 2], jp), MULT)
+        acc = [psum.tile([P, PACK, P], F32, name=f"acc{jt}") for jt in range(J_TILES)]
+        y_codes = keep.tile([P, S], U32, name="y_codes", align_bytes=64)
+        y_scales = keep.tile([P, S], U8, name="y_scales", align_bytes=64)
+        out_rows = out_0.rearrange("(p t) j -> p t j", t=PACK)
+        store_groups = ((0, 1), (2,), (3,))
+        y = {}
+        for group in store_groups:
+            tile = keep.tile([P, PACK, len(group) * P], F32, name=f"y{group[0]}")
+            for jt in group:
+                y[jt] = (tile, group)
 
-        acc = {(h, jp): psum.tile([P, PACK, P], F32, name=f"acc{h}{jp}") for h in range(2) for jp in range(2)}
-        y = [keep.tile([P, PACK, 2 * P], F32, name=f"y{h}") for h in range(2)]
-        y_codes = keep.tile([P, 2 * HALF], U32, name="y_codes", align_bytes=64)
-        y_scales = keep.tile([P, 2 * HALF], U8, name="y_scales", align_bytes=64)
-        store_queue = (nc.sync, nc.scalar)
-
-        def add_up(k):
-            pair, factor, h = steps[k]
-            for jp in range(2):
-                for t in range(PACK):
+        def add_up(k, jps):
+            h = k % 2
+            for jt in [2 * jp + s for jp in jps for s in range(2)]:
+                for u in range(2):
                     nc.tensor.matmul(
-                        acc[h, jp][:, t, :],
-                        lhsT=prod[k][:, jp * N + t * P : jp * N + (t + 1) * P],
+                        acc[jt][:, 2 * h + u, :],
+                        lhsT=prod[k][:, jt * HALF + u * P : jt * HALF + (u + 1) * P],
                         rhs=ident[:],
                         is_transpose=True,
-                        start=(pair == 0 and t == 0),
-                        stop=(pair == 2 and t == PACK - 1),
+                        start=(k == 2 and u == 0),
+                        stop=(k == n_steps - 1 and u == 1),
                     )
-                if pair == 2:
-                    hand_out(h, jp)
+                if k == n_steps - 1:
+                    hand_out(jt)
 
-        def hand_out(h, jp):
-            mine = y[h][:, :, jp * P : (jp + 1) * P]
-            nc.scalar.copy(mine, acc[h, jp][:])
-            y_grouped = keep.tile([P, P * PACK], BF16, name=f"y_grouped{h}{jp}", align_bytes=64)
+        def hand_out(jt):
+            tile, group = y[jt]
+            mine = tile[:, :, (jt - group[0]) * P : (jt - group[0] + 1) * P]
+            nc.scalar.copy(mine, acc[jt][:])
+            if jt == group[-1]:
+                nc.sync.dma_start(out_rows[:, :, group[0] * P : (jt + 1) * P], tile[:])
+            y_grouped = keep.tile([P, P * PACK], BF16, name=f"y_grouped{jt}", align_bytes=64)
             nc.vector.tensor_copy(
                 y_grouped[:].rearrange("p (c i t) -> p c t i", i=4, t=PACK), mine.rearrange("p t (c i) -> p c t i", i=4)
             )
-            cols = slice((2 * h + jp) * P, (2 * h + jp + 1) * P)
+            cols = slice(jt * P, (jt + 1) * P)
             nc.vector.quantize_mx(out=y_codes[:, cols].bitcast(FP8X4), scales=y_scales[:, cols], in_=y_grouped[:])
-            if jp == 1:
-                rows = out_0[h * HALF : (h + 1) * HALF, :].rearrange("(p t) j -> p t j", t=PACK)
-                for s in range(2):
-                    store_queue[s].dma_start(rows[:, :, s * 2 * P : (s + 1) * 2 * P], y[h][s * WORDS : (s + 1) * WORDS])
 
         gather_scales(small_after[-1])
-        for k in range(-2, len(steps) + 1):
-            if k + 2 <= last:
+        for k in range(-2, n_steps - 2):
+            if k + 2 < n_steps:
                 cast(k + 2)
-                if k + 2 in small_after:
-                    gather_scales(small_after[k + 2])
-                if k + 2 in words_after:
-                    gather_words(words_after[k + 2])
-            if 0 <= k + 1 <= last:
+                i, h = divmod(k + 2, 2)
+                if h == 0 and i in words_after and i == 0:
+                    gather_words(words_after[i])
+                if h == 1:
+                    if i in words_after and i > 0:
+                        gather_words(words_after[i])
+                    if i in small_after:
+                        gather_scales(small_after[i])
+                    if i in words_after_small:
+                        gather_words(words_after_small[i])
+            if 0 <= k + 1 < n_steps:
                 quantize(k + 1)
-            if 0 <= k <= last:
-                use(k)
-            if k >= 1 and steps[k - 1][1] == 1:
-                add_up(k - 1)
+            if 0 <= k < n_steps:
+                use(k, (0, 1))
+            if k >= 1 and (k - 1) % 4 >= 2:
+                add_up(k - 1, (0, 1))
+        quantize(n_steps - 1)
+        for jp in range(2):
+            for k in (n_steps - 2, n_steps - 1):
+                use(k, (jp,))
+            for k in (n_steps - 2, n_steps - 1):
+                add_up(k, (jp,))
 
-        words_out = out_1[0].rearrange("(h p) j t -> p h (j t)", h=2).bitcast(I32)
-        for s in range(2):
-            store_queue[s].dma_start(
-                words_out[:, :, s * 2 * P : (s + 1) * 2 * P],
-                y_codes[s * WORDS : (s + 1) * WORDS, :].bitcast(I32).rearrange("p (h j) -> p h j", h=2),
-            )
-        scales_out = out_2[0].bitcast(I32).rearrange("(h r) j -> r h j", h=2)
+        nc.scalar.dma_start(out_1[0].rearrange("p j t -> p (j t)").bitcast(I32), y_codes[:].bitcast(I32))
         for q in range(4):
-            s, b = divmod(q, 2)
-            store_queue[q % 2].dma_start(
-                scales_out[4 * b : 4 * b + 4, :, s * WORDS : (s + 1) * WORDS],
-                y_scales[32 * q : 32 * q + 4, :].bitcast(I32).rearrange("r (h j) -> r h j", h=2),
+            (nc.sync, nc.scalar)[q % 2].dma_start(
+                out_2[0, 4 * q : 4 * q + 4, :].bitcast(I32), y_scales[32 * q : 32 * q + 4, :].bitcast(I32)
             )

@@ -40,7 +40,7 @@ def tile_picked_yffm_sum_po_kernel(
         weights = [(wcu, "d"), (wuc, "x"), (wui, "x"), (wiu, "e"), (wci, "d"), (wic, "e")]
         last_weight = len(weights) - 1
         n_steps = 2 * len(weights)
-        cast_on_vector = (2, 6, 11)
+        cast_on_vector = (0, 2, 6, 7, 11)
         cast_on_gpsimd = ()
         split = ()
 
@@ -82,18 +82,13 @@ def tile_picked_yffm_sum_po_kernel(
                 for h in range(2):
                     raw[2 * i + h] = whole[:].rearrange("p t (c i) -> p c t i", i=PACK)[:, :, :, 2 * h : 2 * h + 2]
 
-        small_after = {-1: "d", 0: "x", 1: "e"}
-        words_after = {0: "d", 2: "e"}
-        words_after_small = {0: "x"}
+        after_weight = {-1: ["w:d", "s:d"], 0: ["s:x", "w:x", "s:e"], 2: ["w:e"]}
         for i in range(-1, len(weights)):
             if i >= 0:
                 load_weight(i)
-            if i in words_after:
-                load_words(words_after[i])
-            if i in small_after:
-                load_list_and_scales(small_after[i])
-            if i in words_after_small:
-                load_words(words_after_small[i])
+            for what in after_weight.get(i, []):
+                kind, name = what.split(":")
+                (load_list_and_scales if kind == "s" else load_words)(name)
 
         def gather_scales(name):
             tok_scales[name] = keep.tile([P, S], U8, name=f"tok_scales_{name}", align_bytes=64)
@@ -117,12 +112,16 @@ def tile_picked_yffm_sum_po_kernel(
                 nc.scalar.copy(dst, src)
 
         def quantize(k):
-            w_codes[k] = keep.tile([P, HALF], U32, name=f"w_codes{k}", align_bytes=64)
-            w_scales[k] = keep.tile([P, HALF], U8, name=f"w_scales{k}", align_bytes=64)
-            nc.vector.quantize_mx(out=w_codes[k][:].bitcast(FP8X4), scales=w_scales[k][:], in_=grouped[k][:])
+            i, h = divmod(k, 2)
+            if h == 0:
+                w_codes[i] = keep.tile([P, N], U32, name=f"w_codes{i}", tag=f"w_codes{i}", align_bytes=64)
+                w_scales[i] = keep.tile([P, N], U8, name=f"w_scales{i}", align_bytes=64)
+            cols = slice(h * HALF, (h + 1) * HALF)
+            nc.vector.quantize_mx(out=w_codes[i][:, cols].bitcast(FP8X4), scales=w_scales[i][:, cols], in_=grouped[k][:])
 
         def project(k, jp):
             table = weights[k // 2][1]
+            half = slice(k % 2 * HALF, (k % 2 + 1) * HALF)
             bank = psum.tile([P, 2, HALF], F32, name="bank", tag="bank", bufs=4)
             for s in range(2):
                 cols = slice((2 * jp + s) * P, (2 * jp + s + 1) * P)
@@ -130,8 +129,8 @@ def tile_picked_yffm_sum_po_kernel(
                     out=bank[:, s, :],
                     lhsT=tok_codes[table][:, cols].bitcast(FP8X4),
                     lhsT_scale=tok_scales[table][tables[table][3] : P, cols],
-                    rhs=w_codes[k][:].bitcast(FP8X4),
-                    rhs_scale=w_scales[k][:],
+                    rhs=w_codes[k // 2][:, half].bitcast(FP8X4),
+                    rhs_scale=w_scales[k // 2][:, half],
                     start=True,
                     stop=True,
                 )
@@ -141,14 +140,19 @@ def tile_picked_yffm_sum_po_kernel(
             i, h = divmod(k, 2)
             for jp in jps:
                 cols = slice(jp * N, (jp + 1) * N)
-                if i % 2 == 0:
+                if i == last_weight - 1:
+                    if h == 0 and jp == 0:
+                        held[i, "whole"] = keep.tile([P, J_TILES * N], F32, name="held_last", tag=f"round{k + 1}", align_bytes=64)
+                    dst = held[i, "whole"][:, 2 * jp * N : 2 * (jp + 1) * N].rearrange("j (s m) -> j s m", s=2)
+                    nc.scalar.copy(dst[:, :, h * HALF : (h + 1) * HALF], project(k, jp).rearrange("j (s m) -> j s m", s=2))
+                elif i % 2 == 0:
                     if jp == 0:
-                        tag = f"stage{i + 1}" if h == 1 else f"held{k}"
+                        tag = f"held{k}"
                         held[k] = keep.tile([P, 2 * N], F32, name=f"held{k}", tag=tag)
                     nc.scalar.copy(held[k][:, cols], project(k, jp))
                 else:
                     if jp == 0:
-                        tag = f"round{k + 1}" if k + 1 < n_steps else "prod_last"
+                        tag = f"round{k + 1}" if k in (2, 6, 7) else f"prod{k}"
                         prod[k] = keep.tile([P, 2 * N], F32, name=f"prod{k}", tag=tag, align_bytes=64)
                     nc.vector.tensor_tensor(prod[k][:, cols], project(k, jp), held[k - 2][:, cols], MULT)
 
@@ -173,10 +177,8 @@ def tile_picked_yffm_sum_po_kernel(
                         rhs=ident[:],
                         is_transpose=True,
                         start=(k == 2 and u == 0),
-                        stop=(k == n_steps - 1 and u == 1),
+                        stop=False,
                     )
-                if k == n_steps - 1:
-                    hand_out(jt)
 
         def hand_out(jt):
             tile, group = y[jt]
@@ -191,20 +193,16 @@ def tile_picked_yffm_sum_po_kernel(
             cols = slice(jt * P, (jt + 1) * P)
             nc.vector.quantize_mx(out=y_codes[:, cols].bitcast(FP8X4), scales=y_scales[:, cols], in_=y_grouped[:])
 
-        gather_scales(small_after[-1])
+        def gathers(i):
+            for what in after_weight.get(i, []):
+                kind, name = what.split(":")
+                (gather_scales if kind == "s" else gather_words)(name)
+
+        gathers(-1)
         for k in range(-2, n_steps - 2):
-            if k + 2 < n_steps:
-                cast(k + 2)
-                i, h = divmod(k + 2, 2)
-                if h == 0 and i in words_after and i == 0:
-                    gather_words(words_after[i])
-                if h == 1:
-                    if i in words_after and i > 0:
-                        gather_words(words_after[i])
-                    if i in small_after:
-                        gather_scales(small_after[i])
-                    if i in words_after_small:
-                        gather_words(words_after_small[i])
+            cast(k + 2)
+            if k % 2 == 1:
+                gathers((k + 2) // 2)
             if 0 <= k + 1 < n_steps:
                 quantize(k + 1)
             if 0 <= k < n_steps:
@@ -212,11 +210,33 @@ def tile_picked_yffm_sum_po_kernel(
             if k >= 1 and (k - 1) % 4 >= 2:
                 add_up(k - 1, (0, 1))
         quantize(n_steps - 1)
-        for jp in range(2):
-            for k in (n_steps - 2, n_steps - 1):
-                use(k, (jp,))
-            for k in (n_steps - 2, n_steps - 1):
-                add_up(k, (jp,))
+        table = weights[last_weight][1]
+        prod_last = []
+        for jt in range(J_TILES):
+            cols = slice(jt * P, (jt + 1) * P)
+            bank = psum.tile([P, N], F32, name="bank", tag="bank", bufs=4)
+            nc.tensor.matmul_mx(
+                out=bank[:],
+                lhsT=tok_codes[table][:, cols].bitcast(FP8X4),
+                lhsT_scale=tok_scales[table][tables[table][3] : P, cols],
+                rhs=w_codes[last_weight][:].bitcast(FP8X4),
+                rhs_scale=w_scales[last_weight][:],
+                start=True,
+                stop=True,
+            )
+            prod_last.append(keep.tile([P, N], F32, name=f"prod_last{jt}"))
+            nc.vector.tensor_tensor(prod_last[jt][:], bank[:], held[last_weight - 1, "whole"][:, jt * N : (jt + 1) * N], MULT)
+        for jt in range(J_TILES):
+            for t in range(PACK):
+                nc.tensor.matmul(
+                    acc[jt][:, t, :],
+                    lhsT=prod_last[jt][:, t * P : (t + 1) * P],
+                    rhs=ident[:],
+                    is_transpose=True,
+                    start=False,
+                    stop=(t == PACK - 1),
+                )
+            hand_out(jt)
 
         nc.scalar.dma_start(out_1[0].rearrange("p j t -> p (j t)").bitcast(I32), y_codes[:].bitcast(I32))
         for q in range(4):

@@ -58,11 +58,9 @@ def tile_picked_yffm_sum_po_kernel(
             words, scales, idx, row0 = tables[name]
             lists[name] = keep.tile([P, S // 16], U16, name=f"list_{name}")
             nc.sync.dma_start(lists[name][:], idx)
-            for q in range(4):
-                nc.sync.dma_start(
-                    scale_win[name][32 * q + row0 : 32 * q + row0 + 4, :].bitcast(I32),
-                    scales[0, 4 * q : 4 * q + 4, :].bitcast(I32),
-                )
+            rows = scales[0].rearrange("(q r) n -> r q n", r=4)
+            for r in range(4):
+                nc.sync.dma_start(scale_win[name][row0 + r : P : 32, :].bitcast(I32), rows[r].bitcast(I32))
 
         def load_words(name):
             words = tables[name][0]

@@ -18,8 +18,8 @@ K = 512
 N = 512
 S = 512
 HALF = N // 2
-WORDS = HALF // PACK
 J_TILES = S // P
+RUN = 4
 FLOPS = 6 * 2 * K * N * S + 5 * N * S
 
 
@@ -32,210 +32,177 @@ def tile_picked_yffm_sum_po_kernel(
         keep = ctx.enter_context(tc.tile_pool(name="keep", bufs=1))
         psum = ctx.enter_context(tc.psum_pool(name="psum", bufs=1))
 
-        tables = {
-            "d": (d_words, d_scales, cxt, 0),
-            "x": (x_words, x_scales, offs, 4),
-            "e": (e_words, e_scales, item, 8),
-        }
+        tables = {"d": (d_words, d_scales, cxt), "x": (x_words, x_scales, offs), "e": (e_words, e_scales, item)}
+        plane_row = {"d": 0, "x": 4, "e": 8}
         weights = [(wcu, "d"), (wuc, "x"), (wui, "x"), (wiu, "e"), (wci, "d"), (wic, "e")]
-        last_weight = len(weights) - 1
-        n_steps = 2 * len(weights)
-        cast_on_vector = (0, 2, 6, 7, 11)
-        cast_on_gpsimd = ()
-        split = ()
+        last = len(weights) - 1
 
         lists, scale_win, word_win, tok_codes, tok_scales = {}, {}, {}, {}, {}
-        for name, (words, scales, idx, row0) in tables.items():
+        raw, stage_tag, rounded, w_codes, w_scales, held, prod = {}, {}, {}, {}, {}, {}, {}
+
+        for name, (_, scales, _) in tables.items():
             scale_win[name] = keep.tile([P, scales.shape[2]], U8, name=f"scale_win_{name}")
-            nc.vector.memset(scale_win[name][:].bitcast(I32), 0)
-
-        ident = keep.tile([P, P], F32, name="ident")
-        make_identity(nc, ident[:])
-
-        raw, grouped, w_codes, w_scales, held, prod = {}, {}, {}, {}, {}, {}
+            nc.gpsimd.memset(scale_win[name][:].bitcast(I32), 0)
 
         def load_list_and_scales(name):
-            words, scales, idx, row0 = tables[name]
+            _, scales, idx = tables[name]
             lists[name] = keep.tile([P, S // 16], U16, name=f"list_{name}")
             nc.sync.dma_start(lists[name][:], idx)
             rows = scales[0].rearrange("(q r) n -> r q n", r=4)
             for r in range(4):
-                nc.sync.dma_start(scale_win[name][row0 + r : P : 32, :].bitcast(I32), rows[r].bitcast(I32))
+                nc.sync.dma_start(scale_win[name][plane_row[name] + r : P : 32, :].bitcast(I32), rows[r].bitcast(I32))
 
         def load_words(name):
             words = tables[name][0]
             word_win[name] = keep.tile([P, words.shape[2]], U32, name=f"word_win_{name}")
             nc.sync.dma_start(word_win[name][:].bitcast(I32), words[0].rearrange("p n t -> p (n t)").bitcast(I32))
 
-        def load_weight(i):
+        def load_weight(i, h=None):
             rows = weights[i][0].rearrange("(p t) m -> p t m", t=PACK)
-            if i in split:
-                for h in range(2):
-                    part = keep.tile([P, PACK, HALF], F32, name=f"raw{i}_{h}", tag=f"stage{i}" if h == 0 else f"stage{i}b")
-                    nc.sync.dma_start(part[:], rows[:, :, h * HALF : (h + 1) * HALF])
-                    raw[2 * i + h] = part[:]
-            else:
-                whole = keep.tile([P, PACK, N], F32, name=f"raw{i}", tag=f"stage{i}")
+            tag = f"stage{i}_{h}"
+            if h is None:
+                whole = keep.tile([P, PACK, N], F32, name=tag, tag=tag, align_bytes=64)
                 nc.sync.dma_start(whole[:], rows)
-                for h in range(2):
-                    raw[2 * i + h] = whole[:].rearrange("p t (c i) -> p c t i", i=PACK)[:, :, :, 2 * h : 2 * h + 2]
+                for u in range(2):
+                    raw[i, u], stage_tag[i, u] = whole[:, :, u * HALF : (u + 1) * HALF], tag
+            else:
+                part = keep.tile([P, PACK, HALF], F32, name=tag, tag=tag, align_bytes=64)
+                nc.sync.dma_start(part[:], rows[:, :, h * HALF : (h + 1) * HALF])
+                raw[i, h], stage_tag[i, h] = part[:], tag
 
-        after_weight = {-1: ["w:d", "s:d"], 0: ["s:x", "w:x", "s:e"], 2: ["w:e"]}
-        for i in range(-1, len(weights)):
-            if i >= 0:
-                load_weight(i)
-            for what in after_weight.get(i, []):
-                kind, name = what.split(":")
-                (load_list_and_scales if kind == "s" else load_words)(name)
+        load_words("d")
+        load_list_and_scales("d")
+        load_weight(0)
+        load_list_and_scales("x")
+        load_weight(1)
+        load_words("x")
+        load_weight(2)
+        load_list_and_scales("e")
+        for h in range(2):
+            load_weight(3, h)
+        load_words("e")
+        for h in range(2):
+            for i in (last - 1, last):
+                load_weight(i, h)
 
-        def gather_scales(name):
+        ident = keep.tile([P, P], F32, name="ident")
+        make_identity(nc, ident[:])
+
+        def round_copy(engine, dst, src):
+            copy = nc.vector.tensor_copy if engine == "vector" else nc.scalar.copy
+            copy(dst.rearrange("p (c i t) -> p c t i", i=RUN, t=PACK), src.rearrange("p t (c i) -> p c t i", i=RUN))
+
+        def on_vector(i, h):
+            return h == 1 and (stage_tag[i, 0] == stage_tag[i, 1] or i == last)
+
+        for (i, h) in raw:
+            rounded[i, h] = keep.tile([P, HALF * PACK], BF16, name=f"rounded{i}_{h}", tag=f"rounded{i}_{h}", align_bytes=64)
+            round_copy("vector" if on_vector(i, h) else "scalar", rounded[i, h][:], raw[i, h])
+
+        for i in range(len(weights)):
+            w_codes[i] = keep.tile([P, N], U32, name=f"w_codes{i}", align_bytes=64)
+            w_scales[i] = keep.tile([P, N], U8, name=f"w_scales{i}", align_bytes=64)
+        for (i, h) in raw:
+            cols = slice(h * HALF, (h + 1) * HALF)
+            nc.vector.quantize_mx(out=w_codes[i][:, cols].bitcast(FP8X4), scales=w_scales[i][:, cols], in_=rounded[i, h][:])
+
+        for name in tables:
+            tok_codes[name] = keep.tile([P, S], U32, name=f"tok_codes_{name}", align_bytes=64)
             tok_scales[name] = keep.tile([P, S], U8, name=f"tok_scales_{name}", align_bytes=64)
+            pieces = 1 if name == "d" else 2
+            for u in range(pieces):
+                nc.vector.tensor_copy(
+                    tok_codes[name][:, u * S // pieces : (u + 1) * S // pieces],
+                    word_win[name][:].indirect(lists[name][:, u * S // 16 // pieces : (u + 1) * S // 16 // pieces]),
+                )
             nc.vector.tensor_copy(tok_scales[name][:], scale_win[name][:].indirect(lists[name][:]))
 
-        def gather_words(name):
-            tok_codes[name] = keep.tile([P, S], U32, name=f"tok_codes_{name}", align_bytes=64)
-            nc.vector.tensor_copy(tok_codes[name][:], word_win[name][:].indirect(lists[name][:]))
-
-        def cast(k):
-            grouped[k] = keep.tile([P, HALF * PACK], BF16, name=f"grouped{k}", tag=f"round{k}", align_bytes=64)
-            dst = grouped[k][:].rearrange("p (i c t) -> p c t i", i=2, t=PACK)
-            src = raw[k]
-            if k in cast_on_gpsimd:
-                n = P // 2
-                for c in range(2):
-                    nc.gpsimd.tensor_copy(dst[:, c * n : (c + 1) * n], src[:, c * n : (c + 1) * n])
-            elif k in cast_on_vector:
-                nc.vector.tensor_copy(dst, src)
-            else:
-                nc.scalar.copy(dst, src)
-
-        def quantize(k):
-            i, h = divmod(k, 2)
-            if h == 0:
-                w_codes[i] = keep.tile([P, N], U32, name=f"w_codes{i}", tag=f"w_codes{i}", align_bytes=64)
-                w_scales[i] = keep.tile([P, N], U8, name=f"w_scales{i}", align_bytes=64)
-            cols = slice(h * HALF, (h + 1) * HALF)
-            nc.vector.quantize_mx(out=w_codes[i][:, cols].bitcast(FP8X4), scales=w_scales[i][:, cols], in_=grouped[k][:])
-
-        def project(k, jp):
-            table = weights[k // 2][1]
-            half = slice(k % 2 * HALF, (k % 2 + 1) * HALF)
-            bank = psum.tile([P, 2, HALF], F32, name="bank", tag="bank", bufs=4)
-            for s in range(2):
-                cols = slice((2 * jp + s) * P, (2 * jp + s + 1) * P)
-                nc.tensor.matmul_mx(
-                    out=bank[:, s, :],
-                    lhsT=tok_codes[table][:, cols].bitcast(FP8X4),
-                    lhsT_scale=tok_scales[table][tables[table][3] : P, cols],
-                    rhs=w_codes[k // 2][:, half].bitcast(FP8X4),
-                    rhs_scale=w_scales[k // 2][:, half],
-                    start=True,
-                    stop=True,
-                )
-            return bank[:].rearrange("j s m -> j (s m)")
-
-        def use(k, jps):
-            i, h = divmod(k, 2)
-            for jp in jps:
-                cols = slice(jp * N, (jp + 1) * N)
-                if i == last_weight - 1:
-                    if h == 0 and jp == 0:
-                        held[i, "whole"] = keep.tile([P, J_TILES * N], F32, name="held_last", tag=f"round{k + 1}", align_bytes=64)
-                    dst = held[i, "whole"][:, 2 * jp * N : 2 * (jp + 1) * N].rearrange("j (s m) -> j s m", s=2)
-                    nc.scalar.copy(dst[:, :, h * HALF : (h + 1) * HALF], project(k, jp).rearrange("j (s m) -> j s m", s=2))
-                elif i % 2 == 0:
-                    if jp == 0:
-                        tag = f"held{k}"
-                        held[k] = keep.tile([P, 2 * N], F32, name=f"held{k}", tag=tag)
-                    nc.scalar.copy(held[k][:, cols], project(k, jp))
-                else:
-                    if jp == 0:
-                        tag = f"round{k + 1}" if k in (2, 6, 7) else f"prod{k}"
-                        prod[k] = keep.tile([P, 2 * N], F32, name=f"prod{k}", tag=tag, align_bytes=64)
-                    nc.vector.tensor_tensor(prod[k][:, cols], project(k, jp), held[k - 2][:, cols], MULT)
-
-        acc = [psum.tile([P, PACK, P], F32, name=f"acc{jt}") for jt in range(J_TILES)]
-        y_codes = keep.tile([P, S], U32, name="y_codes", align_bytes=64)
-        y_scales = keep.tile([P, S], U8, name="y_scales", align_bytes=64)
-        out_rows = out_0.rearrange("(p t) j -> p t j", t=PACK)
-        store_groups = ((0, 1), (2,), (3,))
-        y = {}
-        for group in store_groups:
-            tile = keep.tile([P, PACK, len(group) * P], F32, name=f"y{group[0]}")
-            for jt in group:
-                y[jt] = (tile, group)
-
-        def add_up(k, jps):
-            h = k % 2
-            for jt in [2 * jp + s for jp in jps for s in range(2)]:
-                for u in range(2):
-                    nc.tensor.matmul(
-                        acc[jt][:, 2 * h + u, :],
-                        lhsT=prod[k][:, jt * HALF + u * P : jt * HALF + (u + 1) * P],
-                        rhs=ident[:],
-                        is_transpose=True,
-                        start=(k == 2 and u == 0),
-                        stop=False,
-                    )
-
-        def hand_out(jt):
-            tile, group = y[jt]
-            mine = tile[:, :, (jt - group[0]) * P : (jt - group[0] + 1) * P]
-            nc.scalar.copy(mine, acc[jt][:])
-            if jt == group[-1]:
-                nc.sync.dma_start(out_rows[:, :, group[0] * P : (jt + 1) * P], tile[:])
-            y_grouped = keep.tile([P, P * PACK], BF16, name=f"y_grouped{jt}", align_bytes=64)
-            nc.vector.tensor_copy(
-                y_grouped[:].rearrange("p (c i t) -> p c t i", i=4, t=PACK), mine.rearrange("p t (c i) -> p c t i", i=4)
-            )
+        def project(out, i, jt, m_cols):
+            table = weights[i][1]
             cols = slice(jt * P, (jt + 1) * P)
-            nc.vector.quantize_mx(out=y_codes[:, cols].bitcast(FP8X4), scales=y_scales[:, cols], in_=y_grouped[:])
-
-        def gathers(i):
-            for what in after_weight.get(i, []):
-                kind, name = what.split(":")
-                (gather_scales if kind == "s" else gather_words)(name)
-
-        gathers(-1)
-        for k in range(-2, n_steps - 2):
-            cast(k + 2)
-            if k % 2 == 1:
-                gathers((k + 2) // 2)
-            if 0 <= k + 1 < n_steps:
-                quantize(k + 1)
-            if 0 <= k < n_steps:
-                use(k, (0, 1))
-            if k >= 1 and (k - 1) % 4 >= 2:
-                add_up(k - 1, (0, 1))
-        quantize(n_steps - 1)
-        table = weights[last_weight][1]
-        prod_last = []
-        for jt in range(J_TILES):
-            cols = slice(jt * P, (jt + 1) * P)
-            bank = psum.tile([P, N], F32, name="bank", tag="bank", bufs=4)
             nc.tensor.matmul_mx(
-                out=bank[:],
+                out=out,
                 lhsT=tok_codes[table][:, cols].bitcast(FP8X4),
-                lhsT_scale=tok_scales[table][tables[table][3] : P, cols],
-                rhs=w_codes[last_weight][:].bitcast(FP8X4),
-                rhs_scale=w_scales[last_weight][:],
+                lhsT_scale=tok_scales[table][plane_row[table] : P, cols],
+                rhs=w_codes[i][:, m_cols].bitcast(FP8X4),
+                rhs_scale=w_scales[i][:, m_cols],
                 start=True,
                 stop=True,
             )
-            prod_last.append(keep.tile([P, N], F32, name=f"prod_last{jt}"))
-            nc.vector.tensor_tensor(prod_last[jt][:], bank[:], held[last_weight - 1, "whole"][:, jt * N : (jt + 1) * N], MULT)
-        for jt in range(J_TILES):
+
+        def take(i, bank_view, pick):
+            if i % 2 == 0:
+                nc.scalar.copy(pick(held[i]), bank_view)
+            else:
+                nc.vector.tensor_tensor(pick(prod[i]), bank_view, pick(held[i - 1]), MULT)
+
+        for i in range(len(weights)):
+            tiles = held if i % 2 == 0 else prod
+            if i % 2 == 0 or i == last:
+                donor = stage_tag[i, 1] if i >= last - 1 else stage_tag[i + 1, 1]
+                whole = keep.tile([P, J_TILES, PACK, P], F32, name=f"factor{i}", tag=donor, align_bytes=64)
+                tiles[i] = {jt: whole[:, jt] for jt in range(J_TILES)}
+                tiles[i]["whole"] = whole
+            else:
+                tiles[i] = {}
+                for jt in range(J_TILES):
+                    tag = f"rounded{i + 1}_0" if (i, jt) == (last - 2, J_TILES - 1) else f"prod{i}_{jt}"
+                    tiles[i][jt] = keep.tile([P, PACK, P], F32, name=f"prod{i}_{jt}", tag=tag, align_bytes=64)[:]
+
+        for i in range(last - 1):
+            for jt in range(J_TILES):
+                bank = psum.tile([P, N], F32, name="bank", tag="bank", bufs=4)
+                project(bank[:], i, jt, slice(0, N))
+                take(i, bank[:].rearrange("j (l t) -> j t l", t=PACK), lambda tiles: tiles[jt])
+        for h in range(2):
+            for i in (last - 1, last):
+                if (i, h) == (last, 1):
+                    for jt in range(J_TILES):
+                        bank = psum.tile([P, HALF], F32, name="bank", tag="bank", bufs=4)
+                        project(bank[:], i, jt, slice(HALF, N))
+                        take(i, bank[:].rearrange("j (l t) -> j t l", t=PACK), lambda tiles: tiles[jt][:, :, P // 2 :])
+                    continue
+                for jp in range(2):
+                    bank = psum.tile([P, 2, HALF], F32, name="bank", tag="bank", bufs=4)
+                    for s in range(2):
+                        project(bank[:, s, :], i, 2 * jp + s, slice(h * HALF, (h + 1) * HALF))
+                    take(
+                        i,
+                        bank[:].rearrange("j s (l t) -> j s t l", t=PACK),
+                        lambda tiles: tiles["whole"][:, 2 * jp : 2 * jp + 2, :, h * P // 2 : (h + 1) * P // 2],
+                    )
+
+        acc = [psum.tile([P, PACK, P], F32, name=f"acc{jt}") for jt in range(J_TILES)]
+
+        def add_up(i, jt):
             for t in range(PACK):
                 nc.tensor.matmul(
-                    acc[jt][:, t, :],
-                    lhsT=prod_last[jt][:, t * P : (t + 1) * P],
-                    rhs=ident[:],
-                    is_transpose=True,
-                    start=False,
-                    stop=(t == PACK - 1),
+                    acc[jt][:, t, :], lhsT=prod[i][jt][:, t, :], rhs=ident[:], is_transpose=True,
+                    start=(i == 1 and t == 0), stop=(i == last and t == PACK - 1),
                 )
-            hand_out(jt)
 
+        for i in range(1, last, 2):
+            for jt in range(J_TILES):
+                add_up(i, jt)
+
+        out_rows = out_0.rearrange("(p t) j -> p t j", t=PACK)
+        y_codes = keep.tile([P, S], U32, name="y_codes", align_bytes=64)
+        y_scales = keep.tile([P, S], U8, name="y_scales", align_bytes=64)
+        y, y_rounded = {}, {}
+        for jt in range(J_TILES):
+            add_up(last, jt)
+            y[jt] = keep.tile([P, PACK, P], F32, name=f"y{jt}")
+            (nc.vector.tensor_copy if jt == 1 else nc.scalar.copy)(y[jt][:], acc[jt][:])
+            nc.sync.dma_start(out_rows[:, :, jt * P : (jt + 1) * P], y[jt][:])
+        for jt in range(J_TILES):
+            y_rounded[jt] = keep.tile([P, P * PACK], BF16, name=f"y_rounded{jt}", align_bytes=64)
+            if jt == J_TILES - 1:
+                nc.scalar.copy(y_rounded[jt][:].rearrange("p (c t) -> p c t", t=PACK), acc[jt][:].rearrange("p t c -> p c t"))
+            else:
+                round_copy("vector", y_rounded[jt][:], y[jt][:])
+        for jt in range(J_TILES):
+            cols = slice(jt * P, (jt + 1) * P)
+            nc.vector.quantize_mx(out=y_codes[:, cols].bitcast(FP8X4), scales=y_scales[:, cols], in_=y_rounded[jt][:])
         nc.scalar.dma_start(out_1[0].rearrange("p j t -> p (j t)").bitcast(I32), y_codes[:].bitcast(I32))
         for q in range(4):
             (nc.sync, nc.scalar)[q % 2].dma_start(

@@ -189,17 +189,19 @@ def tile_picked_yffm_sum_po_kernel(
         y_codes = keep.tile([P, S], U32, name="y_codes", align_bytes=64)
         y_scales = keep.tile([P, S], U8, name="y_scales", align_bytes=64)
         y, y_rounded = {}, {}
-        for jt in range(J_TILES):
-            add_up(last, jt)
-            y[jt] = keep.tile([P, PACK, P], F32, name=f"y{jt}")
-            (nc.vector.tensor_copy if jt == 1 else nc.scalar.copy)(y[jt][:], acc[jt][:])
-            nc.sync.dma_start(out_rows[:, :, jt * P : (jt + 1) * P], y[jt][:])
+        for group in ((0,), (1, 2), (3,)):
+            out_tile = keep.tile([P, PACK, len(group) * P], F32, name=f"y{group[0]}")
+            for s, jt in enumerate(group):
+                add_up(last, jt)
+                y[jt] = out_tile[:, :, s * P : (s + 1) * P]
+                (nc.vector.tensor_copy if jt == 1 else nc.scalar.copy)(y[jt], acc[jt][:])
+            nc.sync.dma_start(out_rows[:, :, group[0] * P : (group[-1] + 1) * P], out_tile[:])
         for jt in range(J_TILES):
             y_rounded[jt] = keep.tile([P, P * PACK], BF16, name=f"y_rounded{jt}", align_bytes=64)
             if jt == J_TILES - 1:
                 nc.scalar.copy(y_rounded[jt][:].rearrange("p (c t) -> p c t", t=PACK), acc[jt][:].rearrange("p t c -> p c t"))
             else:
-                round_copy("vector", y_rounded[jt][:], y[jt][:])
+                round_copy("vector", y_rounded[jt][:], y[jt])
         for jt in range(J_TILES):
             cols = slice(jt * P, (jt + 1) * P)
             nc.vector.quantize_mx(out=y_codes[:, cols].bitcast(FP8X4), scales=y_scales[:, cols], in_=y_rounded[jt][:])

@@ -20,6 +20,7 @@ S = 512
 HALF = N // 2
 J_TILES = S // P
 RUN = 4
+SPLIT = 384
 FLOPS = 6 * 2 * K * N * S + 5 * N * S
 
 
@@ -156,56 +157,63 @@ def tile_picked_yffm_sum_po_kernel(
                 take(i, bank[:].rearrange("j (l t) -> j t l", t=PACK), lambda tiles: tiles[jt])
         for h in range(2):
             for i in (last - 1, last):
-                if (i, h) == (last, 1):
-                    for jt in range(J_TILES):
-                        bank = psum.tile([P, HALF], F32, name="bank", tag="bank", bufs=4)
-                        project(bank[:], i, jt, slice(HALF, N))
-                        take(i, bank[:].rearrange("j (l t) -> j t l", t=PACK), lambda tiles: tiles[jt][:, :, P // 2 :])
-                    continue
+                banks = []
                 for jp in range(2):
                     bank = psum.tile([P, 2, HALF], F32, name="bank", tag="bank", bufs=4)
                     for s in range(2):
                         project(bank[:, s, :], i, 2 * jp + s, slice(h * HALF, (h + 1) * HALF))
-                    take(
-                        i,
-                        bank[:].rearrange("j s (l t) -> j s t l", t=PACK),
-                        lambda tiles: tiles["whole"][:, 2 * jp : 2 * jp + 2, :, h * P // 2 : (h + 1) * P // 2],
-                    )
+                    banks.append(bank[:].rearrange("j s (l t) -> j s t l", t=PACK))
+                width = 2 if (i, h) == (last, 1) else PACK
+                for t0 in range(0, PACK, width):
+                    for jp in range(2):
+                        take(
+                            i,
+                            banks[jp][:, :, t0 : t0 + width],
+                            lambda tiles: tiles["whole"][:, 2 * jp : 2 * jp + 2, t0 : t0 + width, h * P // 2 : (h + 1) * P // 2],
+                        )
 
-        acc = [psum.tile([P, PACK, P], F32, name=f"acc{jt}") for jt in range(J_TILES)]
+        acc = {(u, jp): psum.tile([P, 2, HALF], F32, name=f"acc{u}{jp}") for u in range(2) for jp in range(2)}
 
-        def add_up(i, jt):
-            for t in range(PACK):
-                nc.tensor.matmul(
-                    acc[jt][:, t, :], lhsT=prod[i][jt][:, t, :], rhs=ident[:], is_transpose=True,
-                    start=(i == 1 and t == 0), stop=(i == last and t == PACK - 1),
-                )
+        def add_up(i, jt, t):
+            nc.tensor.matmul(
+                acc[t // 2, jt // 2][:, t % 2, jt % 2 * P : (jt % 2 + 1) * P], lhsT=prod[i][jt][:, t, :], rhs=ident[:],
+                is_transpose=True, start=(i == 1 and jt % 2 == 0 and t % 2 == 0), stop=(i == last and jt % 2 == 1 and t % 2 == 1),
+            )
 
         for i in range(1, last, 2):
             for jt in range(J_TILES):
-                add_up(i, jt)
+                for t in range(PACK):
+                    add_up(i, jt, t)
 
         out_rows = out_0.rearrange("(p t) j -> p t j", t=PACK)
+        y = keep.tile([P, PACK, S], F32, name="y")
+        for u in range(2):
+            ts = slice(2 * u, 2 * u + 2)
+            for jp in range(2):
+                js = slice(jp * HALF, (jp + 1) * HALF)
+                for jt in (2 * jp, 2 * jp + 1):
+                    for t in (2 * u, 2 * u + 1):
+                        add_up(last, jt, t)
+                (nc.vector.tensor_copy if (u, jp) == (0, 1) else nc.scalar.copy)(y[:, ts, js], acc[u, jp][:])
+                if u == 0:
+                    nc.sync.dma_start(out_rows[:, ts, js], y[:, ts, js])
+            if u == 1:
+                nc.sync.dma_start(out_rows[:, ts, :], y[:, ts, :])
+
         y_codes = keep.tile([P, S], U32, name="y_codes", align_bytes=64)
         y_scales = keep.tile([P, S], U8, name="y_scales", align_bytes=64)
-        y, y_rounded = {}, {}
-        for group in ((0,), (1, 2), (3,)):
-            out_tile = keep.tile([P, PACK, len(group) * P], F32, name=f"y{group[0]}")
-            for s, jt in enumerate(group):
-                add_up(last, jt)
-                y[jt] = out_tile[:, :, s * P : (s + 1) * P]
-                (nc.vector.tensor_copy if jt == 1 else nc.scalar.copy)(y[jt], acc[jt][:])
-            nc.sync.dma_start(out_rows[:, :, group[0] * P : (group[-1] + 1) * P], out_tile[:])
-        for jt in range(J_TILES):
-            y_rounded[jt] = keep.tile([P, P * PACK], BF16, name=f"y_rounded{jt}", align_bytes=64)
-            if jt == J_TILES - 1:
-                nc.scalar.copy(y_rounded[jt][:].rearrange("p (c t) -> p c t", t=PACK), acc[jt][:].rearrange("p t c -> p c t"))
-            else:
-                round_copy("vector", y_rounded[jt][:], y[jt])
-        for jt in range(J_TILES):
-            cols = slice(jt * P, (jt + 1) * P)
-            nc.vector.quantize_mx(out=y_codes[:, cols].bitcast(FP8X4), scales=y_scales[:, cols], in_=y_rounded[jt][:])
-        nc.scalar.dma_start(out_1[0].rearrange("p j t -> p (j t)").bitcast(I32), y_codes[:].bitcast(I32))
+        y_rounded = keep.tile([P, S * PACK], BF16, name="y_rounded", align_bytes=64)
+        for engine, c0, c1 in (("vector", 0, HALF), ("vector", HALF, SPLIT), ("scalar", SPLIT, S)):
+            round_copy(engine, y_rounded[:, c0 * PACK : c1 * PACK], y[:, :, c0:c1])
+        for h in range(2):
+            cols = slice(h * HALF, (h + 1) * HALF)
+            nc.vector.quantize_mx(
+                out=y_codes[:, cols].bitcast(FP8X4), scales=y_scales[:, cols],
+                in_=y_rounded[:, h * HALF * PACK : (h + 1) * HALF * PACK],
+            )
+            (nc.sync, nc.scalar)[h].dma_start(
+                out_1[0].rearrange("p j t -> p (j t)").bitcast(I32)[:, cols], y_codes[:, cols].bitcast(I32)
+            )
         for q in range(4):
             (nc.sync, nc.scalar)[q % 2].dma_start(
                 out_2[0, 4 * q : 4 * q + 4, :].bitcast(I32), y_scales[32 * q : 32 * q + 4, :].bitcast(I32)

@@ -211,9 +211,7 @@ def tile_picked_yffm_sum_po_kernel(
                 out=y_codes[:, cols].bitcast(FP8X4), scales=y_scales[:, cols],
                 in_=y_rounded[:, h * HALF * PACK : (h + 1) * HALF * PACK],
             )
-            (nc.sync, nc.scalar)[h].dma_start(
-                out_1[0].rearrange("p j t -> p (j t)").bitcast(I32)[:, cols], y_codes[:, cols].bitcast(I32)
-            )
+        nc.scalar.dma_start(out_1[0].rearrange("p j t -> p (j t)").bitcast(I32), y_codes[:].bitcast(I32))
         for q in range(4):
             (nc.sync, nc.scalar)[q % 2].dma_start(
                 out_2[0, 4 * q : 4 * q + 4, :].bitcast(I32), y_scales[32 * q : 32 * q + 4, :].bitcast(I32)

@@ -110,12 +110,9 @@ def tile_picked_yffm_sum_po_kernel(
         for name in tables:
             tok_codes[name] = keep.tile([P, S], U32, name=f"tok_codes_{name}", align_bytes=64)
             tok_scales[name] = keep.tile([P, S], U8, name=f"tok_scales_{name}", align_bytes=64)
-            pieces = 1 if name == "d" else 2
-            for u in range(pieces):
-                nc.vector.tensor_copy(
-                    tok_codes[name][:, u * S // pieces : (u + 1) * S // pieces],
-                    word_win[name][:].indirect(lists[name][:, u * S // 16 // pieces : (u + 1) * S // 16 // pieces]),
-                )
+            cuts = [0, S] if name == "d" else [0, P, 2 * P, S]
+            for j0, j1 in zip(cuts, cuts[1:]):
+                nc.vector.tensor_copy(tok_codes[name][:, j0:j1], word_win[name][:].indirect(lists[name][:, j0 // 16 : j1 // 16]))
             nc.vector.tensor_copy(tok_scales[name][:], scale_win[name][:].indirect(lists[name][:]))
 
         def project(out, i, jt, m_cols):
@@ -164,8 +161,8 @@ def tile_picked_yffm_sum_po_kernel(
                         project(bank[:, s, :], i, 2 * jp + s, slice(h * HALF, (h + 1) * HALF))
                     banks.append(bank[:].rearrange("j s (l t) -> j s t l", t=PACK))
                 width = 2 if (i, h) == (last, 1) else PACK
-                for t0 in range(0, PACK, width):
-                    for jp in range(2):
+                for jp in range(2):
+                    for t0 in range(0, PACK, width):
                         take(
                             i,
                             banks[jp][:, :, t0 : t0 + width],
@@ -187,25 +184,26 @@ def tile_picked_yffm_sum_po_kernel(
 
         out_rows = out_0.rearrange("(p t) j -> p t j", t=PACK)
         y = keep.tile([P, PACK, S], F32, name="y")
-        for u in range(2):
-            ts = slice(2 * u, 2 * u + 2)
-            for jp in range(2):
-                js = slice(jp * HALF, (jp + 1) * HALF)
+        for jp in range(2):
+            js = slice(jp * HALF, (jp + 1) * HALF)
+            for u in range(2):
+                ts = slice(2 * u, 2 * u + 2)
                 for jt in (2 * jp, 2 * jp + 1):
                     for t in (2 * u, 2 * u + 1):
                         add_up(last, jt, t)
-                (nc.vector.tensor_copy if (u, jp) == (0, 1) else nc.scalar.copy)(y[:, ts, js], acc[u, jp][:])
-                if u == 0:
+                (nc.vector.tensor_copy if (u, jp) == (1, 0) else nc.scalar.copy)(y[:, ts, js], acc[u, jp][:])
+                if jp == 0:
                     nc.sync.dma_start(out_rows[:, ts, js], y[:, ts, js])
-            if u == 1:
-                nc.sync.dma_start(out_rows[:, ts, :], y[:, ts, :])
+            if jp == 1:
+                nc.sync.dma_start(out_rows[:, :, js], y[:, :, js])
 
         y_codes = keep.tile([P, S], U32, name="y_codes", align_bytes=64)
         y_scales = keep.tile([P, S], U8, name="y_scales", align_bytes=64)
         y_rounded = keep.tile([P, S * PACK], BF16, name="y_rounded", align_bytes=64)
-        for engine, c0, c1 in (("vector", 0, HALF), ("vector", HALF, SPLIT), ("scalar", SPLIT, S)):
-            round_copy(engine, y_rounded[:, c0 * PACK : c1 * PACK], y[:, :, c0:c1])
+        shares = [[("vector", 0, HALF)], [("vector", HALF, SPLIT), ("scalar", SPLIT, S)]]
         for h in range(2):
+            for engine, c0, c1 in shares[h]:
+                round_copy(engine, y_rounded[:, c0 * PACK : c1 * PACK], y[:, :, c0:c1])
             cols = slice(h * HALF, (h + 1) * HALF)
             nc.vector.quantize_mx(
                 out=y_codes[:, cols].bitcast(FP8X4), scales=y_scales[:, cols],

@@ -11,6 +11,7 @@ U16 = mybir.dt.uint16
 U8 = mybir.dt.uint8
 FP8X4 = mybir.dt.float8_e4m3fn_x4
 MULT = mybir.AluOpType.mult
+ADD = mybir.AluOpType.add
 
 P = 128
 PACK = 4
@@ -98,7 +99,12 @@ def tile_picked_yffm_sum_po_kernel(
 
         for (i, h) in raw:
             rounded[i, h] = keep.tile([P, HALF * PACK], BF16, name=f"rounded{i}_{h}", tag=f"rounded{i}_{h}", align_bytes=64)
-            round_copy("vector" if on_vector(i, h) else "scalar", rounded[i, h][:], raw[i, h])
+            if (i, h) == (last - 1, 0):
+                nc.gpsimd.tensor_scalar(
+                    rounded[i, h][:].rearrange("p (c t) -> p c t", t=PACK), raw[i, h].rearrange("p t c -> p c t"), 1.0, 0.0, MULT, ADD
+                )
+            else:
+                round_copy("vector" if on_vector(i, h) else "scalar", rounded[i, h][:], raw[i, h])
 
         for i in range(len(weights)):
             w_codes[i] = keep.tile([P, N], U32, name=f"w_codes{i}", align_bytes=64)
@@ -137,7 +143,7 @@ def tile_picked_yffm_sum_po_kernel(
         for i in range(len(weights)):
             tiles = held if i % 2 == 0 else prod
             if i % 2 == 0 or i == last:
-                donor = stage_tag[i, 1] if i >= last - 1 else stage_tag[i + 1, 1]
+                donor = {last - 1: stage_tag[last, 0], last: "last_prod"}.get(i) or stage_tag[i + 1, 1]
                 whole = keep.tile([P, J_TILES, PACK, P], F32, name=f"factor{i}", tag=donor, align_bytes=64)
                 tiles[i] = {jt: whole[:, jt] for jt in range(J_TILES)}
                 tiles[i]["whole"] = whole
@@ -162,7 +168,7 @@ def tile_picked_yffm_sum_po_kernel(
                     banks.append(bank[:].rearrange("j s (l t) -> j s t l", t=PACK))
                 width = 2 if (i, h) == (last, 1) else PACK
                 for jp in range(2):
-                    for t0 in range(0, PACK, width):
+                    for t0 in sorted(range(0, PACK, width), reverse=jp == 1):
                         take(
                             i,
                             banks[jp][:, :, t0 : t0 + width],
@@ -186,16 +192,16 @@ def tile_picked_yffm_sum_po_kernel(
         y = keep.tile([P, PACK, S], F32, name="y")
         for jp in range(2):
             js = slice(jp * HALF, (jp + 1) * HALF)
-            for u in range(2):
+            for u in (jp, 1 - jp):
                 ts = slice(2 * u, 2 * u + 2)
                 for jt in (2 * jp, 2 * jp + 1):
                     for t in (2 * u, 2 * u + 1):
                         add_up(last, jt, t)
                 (nc.vector.tensor_copy if (u, jp) == (1, 0) else nc.scalar.copy)(y[:, ts, js], acc[u, jp][:])
-                if jp == 0:
+                if u == 0:
                     nc.sync.dma_start(out_rows[:, ts, js], y[:, ts, js])
-            if jp == 1:
-                nc.sync.dma_start(out_rows[:, :, js], y[:, :, js])
+                elif jp == 1:
+                    nc.sync.dma_start(out_rows[:, ts, :], y[:, ts, :])
 
         y_codes = keep.tile([P, S], U32, name="y_codes", align_bytes=64)
         y_scales = keep.tile([P, S], U8, name="y_scales", align_bytes=64)

@@ -11,7 +11,6 @@ U16 = mybir.dt.uint16
 U8 = mybir.dt.uint8
 FP8X4 = mybir.dt.float8_e4m3fn_x4
 MULT = mybir.AluOpType.mult
-ADD = mybir.AluOpType.add
 
 P = 128
 PACK = 4
@@ -22,6 +21,7 @@ HALF = N // 2
 J_TILES = S // P
 RUN = 4
 SPLIT = 384
+LATE_CUT = 128
 FLOPS = 6 * 2 * K * N * S + 5 * N * S
 
 
@@ -80,12 +80,11 @@ def tile_picked_yffm_sum_po_kernel(
         load_words("x")
         load_weight(2)
         load_list_and_scales("e")
-        for h in range(2):
-            load_weight(3, h)
+        load_weight(3)
         load_words("e")
+        load_weight(last - 1)
         for h in range(2):
-            for i in (last - 1, last):
-                load_weight(i, h)
+            load_weight(last, h)
 
         ident = keep.tile([P, P], F32, name="ident")
         make_identity(nc, ident[:])
@@ -94,17 +93,13 @@ def tile_picked_yffm_sum_po_kernel(
             copy = nc.vector.tensor_copy if engine == "vector" else nc.scalar.copy
             copy(dst.rearrange("p (c i t) -> p c t i", i=RUN, t=PACK), src.rearrange("p t (c i) -> p c t i", i=RUN))
 
-        def on_vector(i, h):
-            return h == 1 and (stage_tag[i, 0] == stage_tag[i, 1] or i == last)
-
         for (i, h) in raw:
             rounded[i, h] = keep.tile([P, HALF * PACK], BF16, name=f"rounded{i}_{h}", tag=f"rounded{i}_{h}", align_bytes=64)
-            if (i, h) == (last - 1, 0):
-                nc.gpsimd.tensor_scalar(
-                    rounded[i, h][:].rearrange("p (c t) -> p c t", t=PACK), raw[i, h].rearrange("p t c -> p c t"), 1.0, 0.0, MULT, ADD
-                )
-            else:
-                round_copy("vector" if on_vector(i, h) else "scalar", rounded[i, h][:], raw[i, h])
+            cut = HALF if h == 0 else LATE_CUT if i == 3 else 0
+            if cut > 0:
+                round_copy("scalar", rounded[i, h][:, : cut * PACK], raw[i, h][:, :, :cut])
+            if cut < HALF:
+                round_copy("vector", rounded[i, h][:, cut * PACK :], raw[i, h][:, :, cut:])
 
         for i in range(len(weights)):
             w_codes[i] = keep.tile([P, N], U32, name=f"w_codes{i}", align_bytes=64)
@@ -143,37 +138,34 @@ def tile_picked_yffm_sum_po_kernel(
         for i in range(len(weights)):
             tiles = held if i % 2 == 0 else prod
             if i % 2 == 0 or i == last:
-                donor = {last - 1: stage_tag[last, 0], last: "last_prod"}.get(i) or stage_tag[i + 1, 1]
+                donor = "last_prod" if i == last else stage_tag[i + 1, 0]
                 whole = keep.tile([P, J_TILES, PACK, P], F32, name=f"factor{i}", tag=donor, align_bytes=64)
                 tiles[i] = {jt: whole[:, jt] for jt in range(J_TILES)}
                 tiles[i]["whole"] = whole
             else:
                 tiles[i] = {}
                 for jt in range(J_TILES):
-                    tag = f"rounded{i + 1}_0" if (i, jt) == (last - 2, J_TILES - 1) else f"prod{i}_{jt}"
+                    tag = f"rounded{i + jt - 1}_0" if i == last - 2 and jt >= 2 else f"prod{i}_{jt}"
                     tiles[i][jt] = keep.tile([P, PACK, P], F32, name=f"prod{i}_{jt}", tag=tag, align_bytes=64)[:]
 
         for i in range(last - 1):
             for jt in range(J_TILES):
-                bank = psum.tile([P, N], F32, name="bank", tag="bank", bufs=4)
+                bank = psum.tile([P, N], F32, name="bank", tag=f"bank{jt}")
                 project(bank[:], i, jt, slice(0, N))
                 take(i, bank[:].rearrange("j (l t) -> j t l", t=PACK), lambda tiles: tiles[jt])
-        for h in range(2):
-            for i in (last - 1, last):
-                banks = []
-                for jp in range(2):
-                    bank = psum.tile([P, 2, HALF], F32, name="bank", tag="bank", bufs=4)
-                    for s in range(2):
-                        project(bank[:, s, :], i, 2 * jp + s, slice(h * HALF, (h + 1) * HALF))
-                    banks.append(bank[:].rearrange("j s (l t) -> j s t l", t=PACK))
-                width = 2 if (i, h) == (last, 1) else PACK
-                for jp in range(2):
-                    for t0 in sorted(range(0, PACK, width), reverse=jp == 1):
-                        take(
-                            i,
-                            banks[jp][:, :, t0 : t0 + width],
-                            lambda tiles: tiles["whole"][:, 2 * jp : 2 * jp + 2, t0 : t0 + width, h * P // 2 : (h + 1) * P // 2],
-                        )
+        steps = [(last - 1, jp, 1 - n) for jp in range(2) for n in range(2)] + [(last, jp, h) for jp in range(2) for h in range(2)]
+        for n, (i, jp, h) in enumerate(steps):
+            bank = psum.tile([P, 2, HALF], F32, name="bank", tag=f"bank{n % 3 if n < 6 else (n + 1) % 4}")
+            for s in range(2):
+                project(bank[:, s, :], i, 2 * jp + s, slice(h * HALF, (h + 1) * HALF))
+            dealt = bank[:].rearrange("j s (l t) -> j s t l", t=PACK)
+            width = 2 if (i, h) == (last, 1) else PACK
+            for t0 in sorted(range(0, PACK, width), reverse=jp == 1):
+                take(
+                    i,
+                    dealt[:, :, t0 : t0 + width],
+                    lambda tiles: tiles["whole"][:, 2 * jp : 2 * jp + 2, t0 : t0 + width, h * P // 2 : (h + 1) * P // 2],
+                )
 
         acc = {(u, jp): psum.tile([P, 2, HALF], F32, name=f"acc{u}{jp}") for u in range(2) for jp in range(2)}
 

@@ -93,20 +93,27 @@ def tile_picked_yffm_sum_po_kernel(
             copy = nc.vector.tensor_copy if engine == "vector" else nc.scalar.copy
             copy(dst.rearrange("p (c i t) -> p c t i", i=RUN, t=PACK), src.rearrange("p t (c i) -> p c t i", i=RUN))
 
+        def pieces(i, h, cut):
+            return [(0, P), (P, HALF)] if (i, h) == (last - 1, 1) else [(cut, HALF)]
+
         for (i, h) in raw:
             rounded[i, h] = keep.tile([P, HALF * PACK], BF16, name=f"rounded{i}_{h}", tag=f"rounded{i}_{h}", align_bytes=64)
             cut = HALF if h == 0 else LATE_CUT if i == 3 else 0
             if cut > 0:
                 round_copy("scalar", rounded[i, h][:, : cut * PACK], raw[i, h][:, :, :cut])
             if cut < HALF:
-                round_copy("vector", rounded[i, h][:, cut * PACK :], raw[i, h][:, :, cut:])
+                for c0, c1 in pieces(i, h, cut):
+                    round_copy("vector", rounded[i, h][:, c0 * PACK : c1 * PACK], raw[i, h][:, :, c0:c1])
 
         for i in range(len(weights)):
             w_codes[i] = keep.tile([P, N], U32, name=f"w_codes{i}", align_bytes=64)
             w_scales[i] = keep.tile([P, N], U8, name=f"w_scales{i}", align_bytes=64)
         for (i, h) in raw:
-            cols = slice(h * HALF, (h + 1) * HALF)
-            nc.vector.quantize_mx(out=w_codes[i][:, cols].bitcast(FP8X4), scales=w_scales[i][:, cols], in_=rounded[i, h][:])
+            for c0, c1 in pieces(i, h, 0):
+                cols = slice(h * HALF + c0, h * HALF + c1)
+                nc.vector.quantize_mx(
+                    out=w_codes[i][:, cols].bitcast(FP8X4), scales=w_scales[i][:, cols], in_=rounded[i, h][:, c0 * PACK : c1 * PACK]
+                )
 
         for name in tables:
             tok_codes[name] = keep.tile([P, S], U32, name=f"tok_codes_{name}", align_bytes=64)
@@ -189,7 +196,7 @@ def tile_picked_yffm_sum_po_kernel(
                 for jt in (2 * jp, 2 * jp + 1):
                     for t in (2 * u, 2 * u + 1):
                         add_up(last, jt, t)
-                (nc.vector.tensor_copy if (u, jp) == (1, 0) else nc.scalar.copy)(y[:, ts, js], acc[u, jp][:])
+                (nc.vector.tensor_copy if (u, jp) == (1, 1) else nc.scalar.copy)(y[:, ts, js], acc[u, jp][:])
                 if u == 0:
                     nc.sync.dma_start(out_rows[:, ts, js], y[:, ts, js])
                 elif jp == 1:
@@ -197,11 +204,10 @@ def tile_picked_yffm_sum_po_kernel(
 
         y_codes = keep.tile([P, S], U32, name="y_codes", align_bytes=64)
         y_scales = keep.tile([P, S], U8, name="y_scales", align_bytes=64)
-        y_rounded = keep.tile([P, S * PACK], BF16, name="y_rounded", align_bytes=64)
-        shares = [[("vector", 0, HALF)], [("vector", HALF, SPLIT), ("scalar", SPLIT, S)]]
+        y_rounded = keep.tile([P, S * PACK], BF16, name="y_rounded", tag="last_prod", align_bytes=64)
+        for engine, c0, c1 in (("vector", 0, HALF), ("vector", HALF, SPLIT), ("scalar", SPLIT, S)):
+            round_copy(engine, y_rounded[:, c0 * PACK : c1 * PACK], y[:, :, c0:c1])
         for h in range(2):
-            for engine, c0, c1 in shares[h]:
-                round_copy(engine, y_rounded[:, c0 * PACK : c1 * PACK], y[:, :, c0:c1])
             cols = slice(h * HALF, (h + 1) * HALF)
             nc.vector.quantize_mx(
                 out=y_codes[:, cols].bitcast(FP8X4), scales=y_scales[:, cols],

@@ -91,7 +91,7 @@ def tile_picked_yffm_sum_po_kernel(
 
         def round_copy(engine, dst, src):
             copy = nc.vector.tensor_copy if engine == "vector" else nc.scalar.copy
-            copy(dst.rearrange("p (c i t) -> p c t i", i=RUN, t=PACK), src.rearrange("p t (c i) -> p c t i", i=RUN))
+            copy(dst.rearrange("p (c i u e) -> p c u i e", i=RUN, u=2, e=2), src.rearrange("p (u e) (c i) -> p c u i e", i=RUN, e=2))
 
         def pieces(i, h, cut):
             return [(0, P), (P, HALF)] if (i, h) == (last - 1, 1) else [(cut, HALF)]

from contextlib import ExitStack

import concourse.mybir as mybir
from concourse.masks import make_identity

F32 = mybir.dt.float32
BF16 = mybir.dt.bfloat16
I32 = mybir.dt.int32
U32 = mybir.dt.uint32
U16 = mybir.dt.uint16
U8 = mybir.dt.uint8
FP8X4 = mybir.dt.float8_e4m3fn_x4
MULT = mybir.AluOpType.mult

P = 128
PACK = 4
K = 512
N = 512
S = 512
HALF = N // 2
J_TILES = S // P
RUN = 4
SPLIT = 384
LATE_CUT = 128
FLOPS = 6 * 2 * K * N * S + 5 * N * S


def tile_picked_yffm_sum_po_kernel(
    tc, x_words, x_scales, e_words, e_scales, d_words, d_scales,
    wui, wuc, wiu, wic, wcu, wci, offs, item, cxt, out_0, out_1, out_2,
):
    nc = tc.nc
    with ExitStack() as ctx:
        keep = ctx.enter_context(tc.tile_pool(name="keep", bufs=1))
        psum = ctx.enter_context(tc.psum_pool(name="psum", bufs=1))

        tables = {"d": (d_words, d_scales, cxt), "x": (x_words, x_scales, offs), "e": (e_words, e_scales, item)}
        plane_row = {"d": 0, "x": 4, "e": 8}
        weights = [(wcu, "d"), (wuc, "x"), (wui, "x"), (wiu, "e"), (wci, "d"), (wic, "e")]
        last = len(weights) - 1

        lists, scale_win, word_win, tok_codes, tok_scales = {}, {}, {}, {}, {}
        raw, stage_tag, rounded, w_codes, w_scales, held, prod = {}, {}, {}, {}, {}, {}, {}

        for name, (_, scales, _) in tables.items():
            scale_win[name] = keep.tile([P, scales.shape[2]], U8, name=f"scale_win_{name}")
            nc.gpsimd.memset(scale_win[name][:].bitcast(I32), 0)

        def load_list_and_scales(name):
            _, scales, idx = tables[name]
            lists[name] = keep.tile([P, S // 16], U16, name=f"list_{name}")
            nc.sync.dma_start(lists[name][:], idx)
            rows = scales[0].rearrange("(q r) n -> r q n", r=4)
            for r in range(4):
                nc.sync.dma_start(scale_win[name][plane_row[name] + r : P : 32, :].bitcast(I32), rows[r].bitcast(I32))

        def load_words(name):
            words = tables[name][0]
            word_win[name] = keep.tile([P, words.shape[2]], U32, name=f"word_win_{name}")
            nc.sync.dma_start(word_win[name][:].bitcast(I32), words[0].rearrange("p n t -> p (n t)").bitcast(I32))

        def load_weight(i, h=None):
            rows = weights[i][0].rearrange("(p t) m -> p t m", t=PACK)
            tag = f"stage{i}_{h}"
            if h is None:
                whole = keep.tile([P, PACK, N], F32, name=tag, tag=tag, align_bytes=64)
                nc.sync.dma_start(whole[:], rows)
                for u in range(2):
                    raw[i, u], stage_tag[i, u] = whole[:, :, u * HALF : (u + 1) * HALF], tag
            else:
                part = keep.tile([P, PACK, HALF], F32, name=tag, tag=tag, align_bytes=64)
                nc.sync.dma_start(part[:], rows[:, :, h * HALF : (h + 1) * HALF])
                raw[i, h], stage_tag[i, h] = part[:], tag

        load_words("d")
        load_list_and_scales("d")
        load_weight(0)
        load_list_and_scales("x")
        load_weight(1)
        load_words("x")
        load_weight(2)
        load_list_and_scales("e")
        load_weight(3)
        load_words("e")
        load_weight(last - 1)
        for h in range(2):
            load_weight(last, h)

        ident = keep.tile([P, P], F32, name="ident")
        make_identity(nc, ident[:])

        def round_copy(engine, dst, src):
            copy = nc.vector.tensor_copy if engine == "vector" else nc.scalar.copy
            copy(dst.rearrange("p (c i u e) -> p c u i e", i=RUN, u=2, e=2), src.rearrange("p (u e) (c i) -> p c u i e", i=RUN, e=2))

        def pieces(i, h, cut):
            return [(0, P), (P, HALF)] if (i, h) == (last - 1, 1) else [(cut, HALF)]

        for (i, h) in raw:
            rounded[i, h] = keep.tile([P, HALF * PACK], BF16, name=f"rounded{i}_{h}", tag=f"rounded{i}_{h}", align_bytes=64)
            cut = HALF if h == 0 else LATE_CUT if i == 3 else 0
            if cut > 0:
                round_copy("scalar", rounded[i, h][:, : cut * PACK], raw[i, h][:, :, :cut])
            if cut < HALF:
                for c0, c1 in pieces(i, h, cut):
                    round_copy("vector", rounded[i, h][:, c0 * PACK : c1 * PACK], raw[i, h][:, :, c0:c1])

        for i in range(len(weights)):
            w_codes[i] = keep.tile([P, N], U32, name=f"w_codes{i}", align_bytes=64)
            w_scales[i] = keep.tile([P, N], U8, name=f"w_scales{i}", align_bytes=64)
        for (i, h) in raw:
            for c0, c1 in pieces(i, h, 0):
                cols = slice(h * HALF + c0, h * HALF + c1)
                nc.vector.quantize_mx(
                    out=w_codes[i][:, cols].bitcast(FP8X4), scales=w_scales[i][:, cols], in_=rounded[i, h][:, c0 * PACK : c1 * PACK]
                )

        for name in tables:
            tok_codes[name] = keep.tile([P, S], U32, name=f"tok_codes_{name}", align_bytes=64)
            tok_scales[name] = keep.tile([P, S], U8, name=f"tok_scales_{name}", align_bytes=64)
            cuts = [0, S] if name == "d" else [0, P, 2 * P, S]
            for j0, j1 in zip(cuts, cuts[1:]):
                nc.vector.tensor_copy(tok_codes[name][:, j0:j1], word_win[name][:].indirect(lists[name][:, j0 // 16 : j1 // 16]))
            nc.vector.tensor_copy(tok_scales[name][:], scale_win[name][:].indirect(lists[name][:]))

        def project(out, i, jt, m_cols):
            table = weights[i][1]
            cols = slice(jt * P, (jt + 1) * P)
            nc.tensor.matmul_mx(
                out=out,
                lhsT=tok_codes[table][:, cols].bitcast(FP8X4),
                lhsT_scale=tok_scales[table][plane_row[table] : P, cols],
                rhs=w_codes[i][:, m_cols].bitcast(FP8X4),
                rhs_scale=w_scales[i][:, m_cols],
                start=True,
                stop=True,
            )

        def take(i, bank_view, pick):
            if i % 2 == 0:
                nc.scalar.copy(pick(held[i]), bank_view)
            else:
                nc.vector.tensor_tensor(pick(prod[i]), bank_view, pick(held[i - 1]), MULT)

        for i in range(len(weights)):
            tiles = held if i % 2 == 0 else prod
            if i % 2 == 0 or i == last:
                donor = "last_prod" if i == last else stage_tag[i + 1, 0]
                whole = keep.tile([P, J_TILES, PACK, P], F32, name=f"factor{i}", tag=donor, align_bytes=64)
                tiles[i] = {jt: whole[:, jt] for jt in range(J_TILES)}
                tiles[i]["whole"] = whole
            else:
                tiles[i] = {}
                for jt in range(J_TILES):
                    tag = f"rounded{i + jt - 1}_0" if i == last - 2 and jt >= 2 else f"prod{i}_{jt}"
                    tiles[i][jt] = keep.tile([P, PACK, P], F32, name=f"prod{i}_{jt}", tag=tag, align_bytes=64)[:]

        for i in range(last - 1):
            for jt in range(J_TILES):
                bank = psum.tile([P, N], F32, name="bank", tag=f"bank{jt}")
                project(bank[:], i, jt, slice(0, N))
                take(i, bank[:].rearrange("j (l t) -> j t l", t=PACK), lambda tiles: tiles[jt])
        steps = [(last - 1, jp, 1 - n) for jp in range(2) for n in range(2)] + [(last, jp, h) for jp in range(2) for h in range(2)]
        for n, (i, jp, h) in enumerate(steps):
            bank = psum.tile([P, 2, HALF], F32, name="bank", tag=f"bank{n % 3 if n < 6 else (n + 1) % 4}")
            for s in range(2):
                project(bank[:, s, :], i, 2 * jp + s, slice(h * HALF, (h + 1) * HALF))
            dealt = bank[:].rearrange("j s (l t) -> j s t l", t=PACK)
            width = 2 if (i, h) == (last, 1) else PACK
            for t0 in sorted(range(0, PACK, width), reverse=jp == 1):
                take(
                    i,
                    dealt[:, :, t0 : t0 + width],
                    lambda tiles: tiles["whole"][:, 2 * jp : 2 * jp + 2, t0 : t0 + width, h * P // 2 : (h + 1) * P // 2],
                )

        acc = {(u, jp): psum.tile([P, 2, HALF], F32, name=f"acc{u}{jp}") for u in range(2) for jp in range(2)}

        def add_up(i, jt, t):
            nc.tensor.matmul(
                acc[t // 2, jt // 2][:, t % 2, jt % 2 * P : (jt % 2 + 1) * P], lhsT=prod[i][jt][:, t, :], rhs=ident[:],
                is_transpose=True, start=(i == 1 and jt % 2 == 0 and t % 2 == 0), stop=(i == last and jt % 2 == 1 and t % 2 == 1),
            )

        for i in range(1, last, 2):
            for jt in range(J_TILES):
                for t in range(PACK):
                    add_up(i, jt, t)

        out_rows = out_0.rearrange("(p t) j -> p t j", t=PACK)
        y = keep.tile([P, PACK, S], F32, name="y")
        for jp in range(2):
            js = slice(jp * HALF, (jp + 1) * HALF)
            for u in (jp, 1 - jp):
                ts = slice(2 * u, 2 * u + 2)
                for jt in (2 * jp, 2 * jp + 1):
                    for t in (2 * u, 2 * u + 1):
                        add_up(last, jt, t)
                (nc.vector.tensor_copy if (u, jp) == (1, 1) else nc.scalar.copy)(y[:, ts, js], acc[u, jp][:])
                if u == 0:
                    nc.sync.dma_start(out_rows[:, ts, js], y[:, ts, js])
                elif jp == 1:
                    nc.sync.dma_start(out_rows[:, ts, :], y[:, ts, :])

        y_codes = keep.tile([P, S], U32, name="y_codes", align_bytes=64)
        y_scales = keep.tile([P, S], U8, name="y_scales", align_bytes=64)
        y_rounded = keep.tile([P, S * PACK], BF16, name="y_rounded", tag="last_prod", align_bytes=64)
        for engine, c0, c1 in (("vector", 0, HALF), ("vector", HALF, SPLIT), ("scalar", SPLIT, S)):
            round_copy(engine, y_rounded[:, c0 * PACK : c1 * PACK], y[:, :, c0:c1])
        for h in range(2):
            cols = slice(h * HALF, (h + 1) * HALF)
            nc.vector.quantize_mx(
                out=y_codes[:, cols].bitcast(FP8X4), scales=y_scales[:, cols],
                in_=y_rounded[:, h * HALF * PACK : (h + 1) * HALF * PACK],
            )
        nc.scalar.dma_start(out_1[0].rearrange("p j t -> p (j t)").bitcast(I32), y_codes[:].bitcast(I32))
        for q in range(4):
            (nc.sync, nc.scalar)[q % 2].dma_start(
                out_2[0, 4 * q : 4 * q + 4, :].bitcast(I32), y_scales[32 * q : 32 * q + 4, :].bitcast(I32)
            )
